import numpy as np
import ml_dtypes


def mxq(x, axis, fmt="e4m3"):
    dtype, down = {"e4m3": (ml_dtypes.float8_e4m3fn, 7), "e5m2": (ml_dtypes.float8_e5m2, 14)}[fmt]
    v = np.moveaxis(np.asarray(x, np.float32).astype(ml_dtypes.bfloat16).astype(np.float64), axis, -1)
    blocks = v.reshape(v.shape[:-1] + (-1, 32))
    amax = np.abs(blocks).max(-1, keepdims=True)
    byte = np.maximum(np.where(amax > 0, np.frexp(amax)[1] - 1 + 127, 0) - down, 1)
    scale = np.exp2(byte - 127.0)
    codes = (blocks / scale).astype(np.float32).astype(dtype).astype(np.float64)
    return np.moveaxis((codes * scale).reshape(v.shape), -1, axis)


WIDE = False


def mx_kscale(k):
    if not WIDE:
        return np.ones(k)
    levels = np.array([10, -10, 5, -5, 0])
    if k % 512:
        return np.exp2(np.random.permutation(np.resize(levels, k // 32))).repeat(32)
    a = np.empty((k // 512, 16))
    for p in range(k // 512):
        a[p, :8] = np.random.permutation(np.resize(levels, 8))
        for g in range(8):
            far = levels[np.abs(levels - a[p, g]) >= 10]
            a[p, g + 8] = far[np.random.randint(len(far))]
    return np.exp2(a.ravel()).repeat(32)


BF16 = ml_dtypes.bfloat16


def bf(x):
    return np.asarray(x, np.float32).astype(BF16)


def f64(x):
    return np.asarray(x).astype(np.float64)


C, G, H, R = 2048, 1024, 512, 256

SLOPE = 0.1


def draw0():
    s, t, u = mx_kscale(G), mx_kscale(H), mx_kscale(C)
    size = np.exp(0.4 * np.random.standard_normal(C))
    return {"x": bf(np.random.standard_normal((C, G)) * size[:, None] * s * u[:, None]),
            "lib": bf(size * u),
            "w_enc": bf(np.random.standard_normal((G, H)) / np.sqrt(G) / s[:, None] * t),
            "b_enc": bf(0.4 * np.random.standard_normal(H) * t),
            "w_dec": bf(np.sqrt(2.0) * np.random.standard_normal((H, G)) / np.sqrt(H) / t[:, None]),
            "b_dec": bf(0.4 * np.random.standard_normal(G)),
            "depth": bf(np.exp(0.4 * np.random.standard_normal(C))),
            "q": bf(np.random.standard_normal((R, C)) / np.sqrt(C) / u),
            "unit": bf(np.exp(0.3 * np.random.standard_normal(H)) / t)}


def core(x, lib, w_enc, b_enc, w_dec, b_dec, depth, q, unit):
    size = f64(lib)[:, None]
    y = (mxq(f64(x), 1, "e4m3") @ mxq(f64(w_enc), 0, "e4m3")) + size * f64(b_enc)[None, :]
    h = np.maximum(y, SLOPE * y)
    d = mxq(h, 1, "e4m3") @ mxq(f64(w_dec), 0, "e4m3")
    z = d / size + f64(b_dec)[None, :]
    mean = f64(depth)[:, None] * np.log(1.0 + np.exp(z))
    k = mxq(f64(q), 1, "e4m3") @ mxq(h, 0, "e4m3")
    contrast = k * f64(unit)[None, :]
    return mean, contrast


def e4m3fn_bytes(y):
    return np.clip(np.asarray(y, np.float64), -448.0, 448.0).astype(np.float32).astype(ml_dtypes.float8_e4m3fn).view(np.uint8)


def e4m3fn_values(b):
    return np.asarray(b, np.uint8).view(ml_dtypes.float8_e4m3fn).astype(np.float64)


def setup_inputs():
    d = draw0()
    x0 = np.asarray(d['w_dec']).astype(np.float64)
    s = (np.max(np.abs(x0), axis=(1,), keepdims=True) / 448.0).astype(np.float32)
    out = {}
    for k, v in d.items():
        if k == 'w_dec':
            out['w_dec_bytes'] = e4m3fn_bytes(x0 / s.astype(np.float64))
            out['w_dec_scale'] = s
        else:
            out[k] = v
    return out


def reference(x, lib, w_enc, b_enc, w_dec_bytes, w_dec_scale, b_dec, depth, q, unit):
    return core(x, lib, w_enc, b_enc, e4m3fn_values(w_dec_bytes) * w_dec_scale.astype(np.float64), b_dec, depth, q, unit)

@@ -1,0 +1,435 @@
+from contextlib import ExitStack
+
+import concourse.mybir as mybir
+from concourse.masks import make_identity
+
+C, G, H, R = 2048, 1024, 512, 256
+FLOPS = 2 * C * G * H + 2 * C * H * G + 2 * R * C * H
+SLOPE = 0.1
+TB, YB, DB = 3, 2, 3
+
+F32 = mybir.dt.float32
+BF16 = mybir.dt.bfloat16
+U32 = mybir.dt.uint32
+U8 = mybir.dt.uint8
+E4M3 = mybir.dt.float8_e4m3fn
+FP8X4 = mybir.dt.float8_e4m3fn_x4
+ALU = mybir.AluOpType
+ACT = mybir.ActivationFunctionType
+
+P = 128
+PACK = 4
+GROUP = P * PACK
+GROUPS = C // GROUP
+KP = G // GROUP
+
+
+def tile_library_size_autoencoder_f6_kernel(
+    tc, x, lib, w_enc, b_enc, w_dec_bytes, w_dec_scale, b_dec, depth, q, unit, out_mean, out_contrast
+):
+    nc = tc.nc
+    with ExitStack() as ctx:
+        keep = ctx.enter_context(tc.tile_pool(name="keep", bufs=1))
+        work = ctx.enter_context(tc.tile_pool(name="work", bufs=2))
+        psum = ctx.enter_context(tc.psum_pool(name="psum", bufs=2))
+        ctx.enter_context(tc.manual_schedule())
+
+        lib_sb = keep.tile([P, GROUPS, PACK], BF16, name="lib_sb")
+        nc.scalar.dma_start(out=lib_sb[:], in_=lib.rearrange("(g p s) -> p g s", p=P, s=PACK))
+        benc_sb = keep.tile([P, PACK], BF16, name="benc_sb")
+        nc.scalar.dma_start(out=benc_sb[:], in_=b_enc.rearrange("(p t) -> p t", t=PACK))
+        wsc_sb = keep.tile([P, PACK], F32, name="wsc_sb")
+        nc.scalar.dma_start(out=wsc_sb[:], in_=w_dec_scale.rearrange("(p t) o -> p (t o)", t=PACK))
+        depth_sb = keep.tile([P, GROUPS, PACK], BF16, name="depth_sb")
+        nc.scalar.dma_start(out=depth_sb[:], in_=depth.rearrange("(g p s) -> p g s", p=P, s=PACK))
+
+        x_view = x.rearrange("(g p s) k -> g p s k", p=P, s=PACK)
+        w_view = w_enc.rearrange("(c p j) n -> c p j n", p=P, j=PACK)
+        x_first = [keep.tile([P, PACK, GROUP], BF16, name="x_first")]
+        x_late = [keep.tile([P, 2, GROUP], BF16, name=f"x_late{half}") for half in range(2)]
+        lib_first = keep.tile([P, GROUP], BF16, name="lib_first")
+        lib_bc = keep.tile([P, C - GROUP], BF16, name="lib_bc")
+        bdec_bc = keep.tile([P, G], BF16, name="bdec_bc")
+        unit_bc = keep.tile([P, H], BF16, name="unit_bc")
+        x_sb = [None] + [keep.tile([P, PACK, G], BF16, name=f"x_sb{g}") for g in range(1, GROUPS)]
+        w_raw = [work.tile([P, PACK, H], BF16, name="w_raw", align_bytes=256) for c in range(KP)]
+        wd_bytes = keep.tile([P, PACK, G], U8, name="wd_bytes")
+        q_sb = keep.tile([P, 2, C], BF16, name="q_sb")
+        for c in range(KP):
+            nc.sync.dma_start(out=w_raw[c][:], in_=w_view[c])
+        nc.sync.dma_start(out=x_first[0][:], in_=x_view[0][:, :, 0:GROUP])
+        for half in range(2):
+            nc.sync.dma_start(
+                out=x_late[half][:], in_=x_view[0][:, 2 * half : 2 * half + 2, GROUP:G]
+            )
+        nc.sync.dma_start(out=wd_bytes[:], in_=w_dec_bytes.rearrange("(p t) g -> p t g", t=PACK))
+        nc.sync.dma_start(out=x_sb[1][:], in_=x_view[1])
+        nc.sync.dma_start(out=bdec_bc[:], in_=b_dec.partition_broadcast(P))
+        nc.sync.dma_start(out=q_sb[:], in_=q.rearrange("(b r) c -> r b c", r=P))
+        nc.sync.dma_start(out=x_sb[2][:], in_=x_view[2])
+        nc.sync.dma_start(out=lib_bc[:], in_=lib[GROUP:C].partition_broadcast(P))
+        nc.sync.dma_start(out=x_sb[3][:], in_=x_view[3])
+        nc.sync.dma_start(out=unit_bc[:], in_=unit.partition_broadcast(P))
+
+        ident32 = keep.tile([P, P], F32, name="ident32")
+        make_identity(nc, ident32[:])
+        ident16 = keep.tile([P, P], BF16, name="ident16")
+        make_identity(nc, ident16[:])
+        warm = keep.tile([P, 1], F32, name="warm")
+        nc.vector.memset(warm[:], 0.0)
+        nc.scalar.activation(out=warm[:], in_=warm[:], func=ACT.Exp)
+        invlib = keep.tile([P, GROUPS, PACK], F32, name="invlib")
+        nc.vector.reciprocal(out=invlib[:], in_=lib_sb[:])
+
+        def spread(columns, out):
+            bank = psum.tile([P, PACK, P], F32, name="tp", bufs=TB)
+            for m in range(PACK):
+                nc.tensor.matmul(
+                    out=bank[:, m, :], lhsT=columns[:, m : m + 1].to_broadcast([P, P]), rhs=ident16[:], start=True, stop=True
+                )
+            nc.scalar.copy(out=out.rearrange("p (m n) -> p m n", m=PACK), in_=bank[:])
+
+        x_grouped = {}
+        x_codes, x_scales = {}, {}
+        we_codes = [keep.tile([P, H], U32, name=f"we_codes{c}", align_bytes=256) for c in range(KP)]
+        we_scales = [keep.tile([P, H], U8, name=f"we_scales{c}", align_bytes=256) for c in range(KP)]
+        wd_codes = keep.tile([P, G], U32, name="wd_codes", align_bytes=256)
+        wd_scales = keep.tile([P, G], U8, name="wd_scales", align_bytes=256)
+
+        def turn_x(g, c, half, engine):
+            bank = psum.tile([P, 2, 2 * P], F32, name="tp", bufs=TB)
+            if g > 0:
+                words = x_sb[g][:, 2 * half : 2 * half + 2, c * GROUP : (c + 1) * GROUP].bitcast(F32)
+            elif c == 0:
+                words = x_first[0][:, 2 * half : 2 * half + 2, :].bitcast(F32)
+            else:
+                words = x_late[half][:].bitcast(F32)
+            for u in (0, 1):
+                for s in (0, 1):
+                    nc.tensor.transpose(
+                        bank[:, u, s * P : (s + 1) * P],
+                        words[:, s, u : 2 * P : 2],
+                        ident32[:],
+                    )
+            if half == 0:
+                x_grouped[g, c] = work.tile([P, GROUP, PACK], BF16, name=f"x_grouped{c}", align_bytes=256)
+            dst = x_grouped[g, c][:].bitcast(F32)[:, half * 256 : (half + 1) * 256, :]
+            src = bank[:].rearrange("p u c -> p c u")
+            if engine == "S":
+                nc.scalar.copy(out=dst, in_=src)
+            else:
+                nc.vector.tensor_copy(out=dst, in_=src)
+
+        def quant_x(g, c, parts=1):
+            x_codes[g, c] = work.tile([P, GROUP], U32, name=f"x_codes{c}", align_bytes=256)
+            x_scales[g, c] = work.tile([P, GROUP], U8, name=f"x_scales{c}", align_bytes=256)
+            width = GROUP // parts
+            for i in range(parts):
+                cols = slice(i * width, (i + 1) * width)
+                nc.vector.quantize_mx(
+                    out=x_codes[g, c][:, cols].bitcast(FP8X4),
+                    scales=x_scales[g, c][:, cols],
+                    in_=x_grouped[g, c][:, cols, :].rearrange("p c j -> p (c j)"),
+                )
+
+        w_grouped = {}
+
+        def group_w(c, lo, hi, engine):
+            if lo == 0:
+                w_grouped[c] = work.tile([P, H, PACK], BF16, name="w_grouped", align_bytes=256)
+            dst = w_grouped[c][:].rearrange("p (t m) j -> p t m j", t=PACK)[:, lo:hi]
+            src = w_raw[c][:].rearrange("p j (m t) -> p t m j", t=PACK)[:, lo:hi]
+            if engine == "S":
+                nc.scalar.copy(out=dst, in_=src)
+            else:
+                nc.vector.tensor_copy(out=dst, in_=src)
+
+        def quant_w(c):
+            nc.vector.quantize_mx(
+                out=we_codes[c][:].bitcast(FP8X4), scales=we_scales[c][:], in_=w_grouped[c][:].rearrange("p c j -> p (c j)")
+            )
+
+        wd_wide = [keep.tile([P, PACK, 512], BF16, name=f"wd_wide{n}") for n in range(2)]
+        wd_grouped = {}
+
+        def widen_wd(n):
+            cols = slice(n * 512, (n + 1) * 512)
+            for t in range(PACK):
+                nc.scalar.activation(
+                    out=wd_wide[n][:, t, :],
+                    in_=wd_bytes[:, t, cols].bitcast(E4M3),
+                    func=ACT.Copy,
+                    scale=wsc_sb[:, t : t + 1],
+                )
+
+        def group_wd(n):
+            cols = slice(n * 512, (n + 1) * 512)
+            wd_grouped[n] = work.tile([P, H, PACK], BF16, name="w_grouped", align_bytes=256)
+            nc.gpsimd.tensor_scalar(
+                out=wd_grouped[n][:],
+                in0=wd_wide[n][:].rearrange("p t g -> p g t"),
+                scalar1=1.0,
+                scalar2=0.0,
+                op0=ALU.mult,
+                op1=ALU.add,
+            )
+
+        def quant_wd(n):
+            cols = slice(n * 512, (n + 1) * 512)
+            nc.vector.quantize_mx(
+                out=wd_codes[:, cols].bitcast(FP8X4),
+                scales=wd_scales[:, cols],
+                in_=wd_grouped[n][:].rearrange("p g t -> p (g t)"),
+            )
+
+        sums = {}
+        h_grouped, h_codes, h_scales = {}, {}, {}
+
+        def encode(g, t):
+            bank = psum.tile([P, GROUP], F32, name="y_bank", bufs=YB)
+            for c in range(KP):
+                nc.tensor.matmul_mx(
+                    out=bank[:],
+                    lhsT=we_codes[c][:, t * P : (t + 1) * P].bitcast(FP8X4),
+                    lhsT_scale=we_scales[c][:, t * P : (t + 1) * P],
+                    rhs=x_codes[g, c][:].bitcast(FP8X4),
+                    rhs_scale=x_scales[g, c][:],
+                    start=(c == 0),
+                    stop=(c == KP - 1),
+                )
+            if t == 0:
+                sums[g] = work.tile([P, PACK, GROUP], F32, name="sums", bufs=1)
+            if g == 0:
+                lib_row = lib_first[:].rearrange("p (s n) -> p s n", s=PACK)
+            else:
+                lib_row = lib_bc[:, (g - 1) * GROUP : g * GROUP].rearrange("p (n s) -> p s n", s=PACK)
+            nc.vector.scalar_tensor_tensor(
+                out=sums[g][:, t, :].rearrange("p (s n) -> p s n", s=PACK),
+                in0=lib_row,
+                scalar=benc_sb[:, t : t + 1],
+                in1=bank[:].rearrange("p (s n) -> p s n", s=PACK),
+                op0=ALU.mult,
+                op1=ALU.add,
+            )
+
+        def leaky(g, part):
+            if part == 0:
+                h_grouped[g] = work.tile([P, GROUP, PACK], BF16, name="h_grouped", align_bytes=256)
+            cols = slice(part * 256, (part + 1) * 256)
+            src = sums[g][:, :, cols].rearrange("p t c -> p c t")
+            nc.vector.scalar_tensor_tensor(
+                out=h_grouped[g][:, cols, :], in0=src, scalar=SLOPE, in1=src, op0=ALU.mult, op1=ALU.max
+            )
+
+        def quant_h(g, part):
+            if part == 0:
+                h_codes[g] = work.tile([P, GROUP], U32, name="h_codes", align_bytes=256)
+                h_scales[g] = work.tile([P, GROUP], U8, name="h_scales", align_bytes=256)
+            cols = slice(part * 256, (part + 1) * 256)
+            nc.vector.quantize_mx(
+                out=h_codes[g][:, cols].bitcast(FP8X4),
+                scales=h_scales[g][:, cols],
+                in_=h_grouped[g][:, cols, :].rearrange("p c t -> p (c t)"),
+            )
+
+        z = {}
+
+        def decode(g, s, n):
+            bank = psum.tile([P, 512], F32, name="d_bank", bufs=DB)
+            nc.tensor.matmul_mx(
+                out=bank[:],
+                lhsT=h_codes[g][:, s * P : (s + 1) * P].bitcast(FP8X4),
+                lhsT_scale=h_scales[g][:, s * P : (s + 1) * P],
+                rhs=wd_codes[:, n * 512 : (n + 1) * 512].bitcast(FP8X4),
+                rhs_scale=wd_scales[:, n * 512 : (n + 1) * 512],
+                start=True,
+                stop=True,
+            )
+            if n == 0:
+                z[g, s] = keep.tile([P, G], F32, name=f"z{g}_{s}")
+            nc.vector.scalar_tensor_tensor(
+                out=z[g, s][:, n * 512 : (n + 1) * 512],
+                in0=bank[:],
+                scalar=invlib[:, g, s : s + 1],
+                in1=bdec_bc[:, n * 512 : (n + 1) * 512],
+                op0=ALU.mult,
+                op1=ALU.add,
+            )
+
+        def exp(g, s):
+            nc.scalar.activation(out=z[g, s][:], in_=z[g, s][:], func=ACT.Exp)
+
+        def log(g, s, lo=0, hi=G):
+            nc.scalar.activation(out=z[g, s][:, lo:hi], in_=z[g, s][:, lo:hi], func=ACT.Ln, bias=1.0)
+
+        mean_view = out_mean.rearrange("(g p s) n -> g s p n", p=P, s=PACK)
+
+        def finish(g, s, lo=0, hi=G):
+            nc.vector.tensor_scalar(
+                out=z[g, s][:, lo:hi], in0=z[g, s][:, lo:hi], scalar1=depth_sb[:, g, s : s + 1], scalar2=None, op0=ALU.mult
+            )
+            nc.sync.dma_start(out=mean_view[g, s][:, lo:hi], in_=z[g, s][:, lo:hi])
+
+        hc_grouped, hc_codes, hc_scales = {}, {}, {}
+
+        def turn_h(g, tt, engine):
+            bank = psum.tile([P, PACK, P], F32, name="tp", bufs=TB)
+            words = h_grouped[g][:].bitcast(F32)
+            for s in range(PACK):
+                nc.tensor.transpose(bank[:, s, :], words[:, s * P : (s + 1) * P, tt : tt + 1].rearrange("p c o -> p (c o)"), ident32[:])
+            if tt == 0:
+                hc_grouped[g] = work.tile([P, H, PACK], BF16, name="w_raw" if g < 2 else "w_grouped", align_bytes=256)
+            dst = hc_grouped[g][:, tt * 256 : (tt + 1) * 256, :]
+            src = bank[:].bitcast(BF16).rearrange("p s c -> p c s")
+            if engine == "S":
+                nc.scalar.copy(out=dst, in_=src)
+            else:
+                nc.vector.tensor_copy(out=dst, in_=src)
+
+        def quant_hc(g):
+            hc_codes[g] = keep.tile([P, H], U32, name=f"hc_codes{g}", align_bytes=256)
+            hc_scales[g] = keep.tile([P, H], U8, name=f"hc_scales{g}", align_bytes=256)
+            nc.vector.quantize_mx(
+                out=hc_codes[g][:].bitcast(FP8X4), scales=hc_scales[g][:], in_=hc_grouped[g][:].rearrange("p c j -> p (c j)")
+            )
+
+        q_grouped, q_codes, q_scales = {}, {}, {}
+
+        def turn_q(g):
+            bank = psum.tile([P, 2, 2 * P], F32, name="tp", bufs=TB)
+            words = q_sb[:].bitcast(F32)
+            for u in (0, 1):
+                for b in (0, 1):
+                    nc.tensor.transpose(
+                        bank[:, u, b * P : (b + 1) * P], words[:, b, 256 * g + u : 256 * (g + 1) : 2], ident32[:]
+                    )
+            q_grouped[g] = work.tile([P, R, PACK], BF16, name="q_grouped", align_bytes=256, bufs=4)
+            nc.scalar.copy(out=q_grouped[g][:].bitcast(F32), in_=bank[:].rearrange("p u c -> p c u"))
+
+        def quant_q(g):
+            q_codes[g] = keep.tile([P, R], U32, name=f"q_codes{g}", align_bytes=256)
+            q_scales[g] = keep.tile([P, R], U8, name=f"q_scales{g}", align_bytes=256)
+            nc.vector.quantize_mx(
+                out=q_codes[g][:].bitcast(FP8X4), scales=q_scales[g][:], in_=q_grouped[g][:].rearrange("p c j -> p (c j)")
+            )
+
+        def contrast(b):
+            bank = psum.tile([P, H], F32, name="d_bank", bufs=DB)
+            for g in range(GROUPS):
+                nc.tensor.matmul_mx(
+                    out=bank[:],
+                    lhsT=q_codes[g][:, b * P : (b + 1) * P].bitcast(FP8X4),
+                    lhsT_scale=q_scales[g][:, b * P : (b + 1) * P],
+                    rhs=hc_codes[g][:].bitcast(FP8X4),
+                    rhs_scale=hc_scales[g][:],
+                    start=(g == 0),
+                    stop=(g == GROUPS - 1),
+                )
+            res = work.tile([P, H], F32, name="contrast_sb")
+            nc.vector.tensor_tensor(
+                out=res[:].rearrange("p (m v e) -> p m v e", v=2, e=2),
+                in0=bank[:].rearrange("p (v m e) -> p m v e", v=2, e=2),
+                in1=unit_bc[:].rearrange("p (m v e) -> p m v e", v=2, e=2),
+                op=ALU.mult,
+            )
+            nc.sync.dma_start(out=out_contrast[b * P : (b + 1) * P, :], in_=res[:])
+
+        tiles = [(g, s) for g in range(GROUPS) for s in range(PACK)]
+        early = 8
+        todo = [(exp, t) for t in tiles[:8]]
+        todo += [(log, t) for t in tiles[:early]]
+        todo += [(exp, t) for t in tiles[8:]]
+        todo += [(log, t) for t in tiles[early:]]
+
+        def fill(n):
+            for i in range(n):
+                stage, (g, s) = todo.pop(0)
+                stage(g, s)
+
+        ready = list(tiles)
+
+        def store(n):
+            for i in range(n):
+                finish(*ready.pop(0))
+
+        spread(lib_sb[:, 0, :], lib_first[:])
+        group_w(0, 0, 2, "V")
+        group_w(0, 2, 4, "S")
+        group_w(1, 0, 4, "V")
+        turn_x(0, 0, 0, "S")
+        quant_w(0)
+        turn_x(0, 0, 1, "S")
+        quant_w(1)
+        turn_x(0, 1, 0, "S")
+        quant_x(0, 0)
+        turn_x(0, 1, 1, "S")
+        quant_x(0, 1, 2)
+        widen_wd(0)
+        widen_wd(1)
+        group_wd(0)
+        group_wd(1)
+        for g in range(GROUPS):
+            last = g == GROUPS - 1
+            for t in range(PACK):
+                encode(g, t)
+            if g > 0:
+                quant_q(g - 1)
+            fill([0,2,2,2][g])
+            if not last:
+                for c in range(KP):
+                    for half in range(2):
+                        turn_x(g + 1, c, half, "S")
+            for k in [[0,1],[2],[],[]][g]:
+                turn_q(k)
+            store([0,0,0,2][g])
+            leaky(g, 0)
+            leaky(g, 1)
+            if g == 0:
+                quant_wd(0)
+            quant_h(g, 0)
+            quant_h(g, 1)
+            if g == 0:
+                quant_wd(1)
+            if not last:
+                quant_x(g + 1, 0)
+            decode(g, 0, 0)
+            decode(g, 0, 1)
+            fill([1,1,1,2][g])
+            decode(g, 1, 0)
+            if g < 3:
+                turn_h(g, 0, "S")
+            decode(g, 1, 1)
+            fill([1,1,1,2][g])
+            decode(g, 2, 0)
+            if not last:
+                quant_x(g + 1, 1)
+            store([0,0,0,2][g])
+            if g < 3:
+                turn_h(g, 1, "S")
+            for k in [[],[],[3],[]][g]:
+                turn_q(k)
+            decode(g, 2, 1)
+            decode(g, 3, 0)
+            decode(g, 3, 1)
+            fill([0,0,1,2][g])
+            store([0,0,0,2][g])
+        rest = []
+        for k in range(3, GROUPS):
+            rest += [lambda k=k: turn_h(k, 0, "V"), lambda k=k: turn_h(k, 1, "V")]
+        rest += [lambda: quant_q(3)]
+        rest += [lambda k=k: quant_hc(k) for k in range(GROUPS)]
+        rest += [lambda b=b: contrast(b) for b in range(2)]
+        while 16 - len(ready) < early:
+            store(1)
+            if rest:
+                rest.pop(0)()
+        for job in rest:
+            job()
+        while len(todo) > 16 - early:
+            fill(1)
+        for i in range(early, 15):
+            fill(1)
+            store(1)
+        for h in range(2):
+            log(3, 3, h * 512, (h + 1) * 512)
+            finish(3, 3, h * 512, (h + 1) * 512)

@@ -81,6 +81,14 @@ def tile_library_size_autoencoder_f6_kernel(
         invlib = keep.tile([P, GROUPS, PACK], F32, name="invlib")
         nc.vector.reciprocal(out=invlib[:], in_=lib_sb[:])
 
+        dummy_in = keep.tile([P, 512], BF16, name="dummy_in")
+        nc.vector.memset(dummy_in[:], 0.0)
+
+        def keep_busy(n):
+            for i in range(n):
+                bank = psum.tile([P, 512], F32, name="d_bank", bufs=DB)
+                nc.tensor.matmul(out=bank[:], lhsT=ident16[:], rhs=dummy_in[:], start=True, stop=True)
+
         def spread(columns, out):
             bank = psum.tile([P, PACK, P], F32, name="tp", bufs=TB)
             for m in range(PACK):
@@ -111,7 +119,7 @@ def tile_library_size_autoencoder_f6_kernel(
                         words[:, s, u : 2 * P : 2],
                         ident32[:],
                     )
-            if half == 0:
+            if (g, c) not in x_grouped:
                 x_grouped[g, c] = work.tile([P, GROUP, PACK], BF16, name=f"x_grouped{c}", align_bytes=256)
             dst = x_grouped[g, c][:].bitcast(F32)[:, half * 256 : (half + 1) * 256, :]
             src = bank[:].rearrange("p u c -> p c u")
@@ -135,7 +143,7 @@ def tile_library_size_autoencoder_f6_kernel(
         w_grouped = {}
 
         def group_w(c, lo, hi, engine):
-            if lo == 0:
+            if c not in w_grouped:
                 w_grouped[c] = work.tile([P, H, PACK], BF16, name="w_grouped", align_bytes=256)
             dst = w_grouped[c][:].rearrange("p (t m) j -> p t m j", t=PACK)[:, lo:hi]
             src = w_raw[c][:].rearrange("p j (m t) -> p t m j", t=PACK)[:, lo:hi]
@@ -162,17 +170,13 @@ def tile_library_size_autoencoder_f6_kernel(
                     scale=wsc_sb[:, t : t + 1],
                 )
 
-        def group_wd(n):
-            cols = slice(n * 512, (n + 1) * 512)
+        def group_wd(n, engine):
             wd_grouped[n] = work.tile([P, H, PACK], BF16, name="w_grouped", align_bytes=256)
-            nc.gpsimd.tensor_scalar(
-                out=wd_grouped[n][:],
-                in0=wd_wide[n][:].rearrange("p t g -> p g t"),
-                scalar1=1.0,
-                scalar2=0.0,
-                op0=ALU.mult,
-                op1=ALU.add,
-            )
+            src = wd_wide[n][:].rearrange("p t g -> p g t")
+            if engine == "S":
+                nc.scalar.copy(out=wd_grouped[n][:], in_=src)
+            else:
+                nc.vector.tensor_copy(out=wd_grouped[n][:], in_=src)
 
         def quant_wd(n):
             cols = slice(n * 512, (n + 1) * 512)
@@ -197,7 +201,7 @@ def tile_library_size_autoencoder_f6_kernel(
                     start=(c == 0),
                     stop=(c == KP - 1),
                 )
-            if t == 0:
+            if g not in sums:
                 sums[g] = work.tile([P, PACK, GROUP], F32, name="sums", bufs=1)
             if g == 0:
                 lib_row = lib_first[:].rearrange("p (s n) -> p s n", s=PACK)
@@ -213,7 +217,7 @@ def tile_library_size_autoencoder_f6_kernel(
             )
 
         def leaky(g, part):
-            if part == 0:
+            if g not in h_grouped:
                 h_grouped[g] = work.tile([P, GROUP, PACK], BF16, name="h_grouped", align_bytes=256)
             cols = slice(part * 256, (part + 1) * 256)
             src = sums[g][:, :, cols].rearrange("p t c -> p c t")
@@ -222,7 +226,7 @@ def tile_library_size_autoencoder_f6_kernel(
             )
 
         def quant_h(g, part):
-            if part == 0:
+            if g not in h_codes:
                 h_codes[g] = work.tile([P, GROUP], U32, name="h_codes", align_bytes=256)
                 h_scales[g] = work.tile([P, GROUP], U8, name="h_scales", align_bytes=256)
             cols = slice(part * 256, (part + 1) * 256)
@@ -234,7 +238,7 @@ def tile_library_size_autoencoder_f6_kernel(
 
         z = {}
 
-        def decode(g, s, n):
+        def decode(g, s, n, engine="V"):
             bank = psum.tile([P, 512], F32, name="d_bank", bufs=DB)
             nc.tensor.matmul_mx(
                 out=bank[:],
@@ -245,7 +249,7 @@ def tile_library_size_autoencoder_f6_kernel(
                 start=True,
                 stop=True,
             )
-            if n == 0:
+            if (g, s) not in z:
                 z[g, s] = keep.tile([P, G], F32, name=f"z{g}_{s}")
             nc.vector.scalar_tensor_tensor(
                 out=z[g, s][:, n * 512 : (n + 1) * 512],
@@ -277,7 +281,7 @@ def tile_library_size_autoencoder_f6_kernel(
             words = h_grouped[g][:].bitcast(F32)
             for s in range(PACK):
                 nc.tensor.transpose(bank[:, s, :], words[:, s * P : (s + 1) * P, tt : tt + 1].rearrange("p c o -> p (c o)"), ident32[:])
-            if tt == 0:
+            if g not in hc_grouped:
                 hc_grouped[g] = work.tile([P, H, PACK], BF16, name="w_raw" if g < 2 else "w_grouped", align_bytes=256)
             dst = hc_grouped[g][:, tt * 256 : (tt + 1) * 256, :]
             src = bank[:].bitcast(BF16).rearrange("p s c -> p c s")
@@ -334,102 +338,196 @@ def tile_library_size_autoencoder_f6_kernel(
             )
             nc.sync.dma_start(out=out_contrast[b * P : (b + 1) * P, :], in_=res[:])
 
-        tiles = [(g, s) for g in range(GROUPS) for s in range(PACK)]
-        early = 8
-        todo = [(exp, t) for t in tiles[:8]]
-        todo += [(log, t) for t in tiles[:early]]
-        todo += [(exp, t) for t in tiles[8:]]
-        todo += [(log, t) for t in tiles[early:]]
-
-        def fill(n):
-            for i in range(n):
-                stage, (g, s) = todo.pop(0)
-                stage(g, s)
-
-        ready = list(tiles)
-
-        def store(n):
-            for i in range(n):
-                finish(*ready.pop(0))
-
-        spread(lib_sb[:, 0, :], lib_first[:])
-        group_w(0, 0, 2, "V")
-        group_w(0, 2, 4, "S")
         group_w(1, 0, 4, "V")
-        turn_x(0, 0, 0, "S")
-        quant_w(0)
-        turn_x(0, 0, 1, "S")
+        keep_busy(1)
+        keep_busy(1)
+        keep_busy(1)
         quant_w(1)
-        turn_x(0, 1, 0, "S")
+        keep_busy(1)
+        spread(lib_sb[:, 0, :], lib_first[:])
+        keep_busy(1)
+        keep_busy(1)
+        keep_busy(1)
+        group_w(0, 2, 4, "S")
+        turn_x(0, 0, 0, "S")
+        turn_x(0, 0, 1, "S")
+        keep_busy(1)
+        group_w(0, 0, 2, "V")
+        keep_busy(1)
         quant_x(0, 0)
-        turn_x(0, 1, 1, "S")
-        quant_x(0, 1, 2)
+        keep_busy(1)
+        quant_w(0)
         widen_wd(0)
+        turn_x(0, 1, 0, "S")
+        keep_busy(1)
+        turn_x(0, 1, 1, "S")
+        group_wd(0, "V")
+        quant_x(0, 1, 2)
+        keep_busy(1)
+        keep_busy(1)
         widen_wd(1)
-        group_wd(0)
-        group_wd(1)
-        for g in range(GROUPS):
-            last = g == GROUPS - 1
-            for t in range(PACK):
-                encode(g, t)
-            if g > 0:
-                quant_q(g - 1)
-            fill([0,2,2,2][g])
-            if not last:
-                for c in range(KP):
-                    for half in range(2):
-                        turn_x(g + 1, c, half, "S")
-            for k in [[0,1],[2],[],[]][g]:
-                turn_q(k)
-            store([0,0,0,2][g])
-            leaky(g, 0)
-            leaky(g, 1)
-            if g == 0:
-                quant_wd(0)
-            quant_h(g, 0)
-            quant_h(g, 1)
-            if g == 0:
-                quant_wd(1)
-            if not last:
-                quant_x(g + 1, 0)
-            decode(g, 0, 0)
-            decode(g, 0, 1)
-            fill([1,1,1,2][g])
-            decode(g, 1, 0)
-            if g < 3:
-                turn_h(g, 0, "S")
-            decode(g, 1, 1)
-            fill([1,1,1,2][g])
-            decode(g, 2, 0)
-            if not last:
-                quant_x(g + 1, 1)
-            store([0,0,0,2][g])
-            if g < 3:
-                turn_h(g, 1, "S")
-            for k in [[],[],[3],[]][g]:
-                turn_q(k)
-            decode(g, 2, 1)
-            decode(g, 3, 0)
-            decode(g, 3, 1)
-            fill([0,0,1,2][g])
-            store([0,0,0,2][g])
-        rest = []
-        for k in range(3, GROUPS):
-            rest += [lambda k=k: turn_h(k, 0, "V"), lambda k=k: turn_h(k, 1, "V")]
-        rest += [lambda: quant_q(3)]
-        rest += [lambda k=k: quant_hc(k) for k in range(GROUPS)]
-        rest += [lambda b=b: contrast(b) for b in range(2)]
-        while 16 - len(ready) < early:
-            store(1)
-            if rest:
-                rest.pop(0)()
-        for job in rest:
-            job()
-        while len(todo) > 16 - early:
-            fill(1)
-        for i in range(early, 15):
-            fill(1)
-            store(1)
-        for h in range(2):
-            log(3, 3, h * 512, (h + 1) * 512)
-            finish(3, 3, h * 512, (h + 1) * 512)
+        keep_busy(1)
+        group_wd(1, "S")
+        keep_busy(1)
+        turn_x(1, 0, 0, "S")
+        encode(0, 1)
+        encode(0, 0)
+        encode(0, 2)
+        encode(0, 3)
+        turn_x(1, 1, 1, "S")
+        leaky(0, 0)
+        turn_x(1, 0, 1, "S")
+        keep_busy(1)
+        quant_wd(1)
+        keep_busy(1)
+        quant_h(0, 0)
+        quant_wd(0)
+        leaky(0, 1)
+        turn_x(1, 1, 0, "S")
+        decode(0, 0, 1, "V")
+        quant_h(0, 1)
+        quant_x(1, 1)
+        decode(0, 1, 1, "V")
+        turn_q(0)
+        turn_h(0, 0, "S")
+        decode(0, 0, 0, "V")
+        turn_h(0, 1, "S")
+        exp(0, 0)
+        decode(0, 1, 0, "V")
+        decode(0, 2, 1, "V")
+        decode(0, 2, 0, "V")
+        quant_x(1, 0)
+        decode(0, 3, 1, "V")
+        exp(0, 1)
+        exp(0, 2)
+        decode(0, 3, 0, "V")
+        turn_x(2, 0, 0, "S")
+        encode(1, 1)
+        encode(1, 0)
+        encode(1, 2)
+        encode(1, 3)
+        turn_x(2, 1, 1, "S")
+        leaky(1, 0)
+        turn_x(2, 0, 1, "S")
+        keep_busy(1)
+        keep_busy(1)
+        quant_h(1, 0)
+        exp(0, 3)
+        quant_q(0)
+        leaky(1, 1)
+        turn_x(2, 1, 0, "S")
+        decode(1, 0, 1, "V")
+        quant_h(1, 1)
+        quant_x(2, 1)
+        decode(1, 1, 1, "V")
+        turn_q(1)
+        turn_h(1, 0, "S")
+        decode(1, 0, 0, "V")
+        turn_h(1, 1, "S")
+        exp(1, 0)
+        decode(1, 1, 0, "V")
+        decode(1, 2, 1, "V")
+        decode(1, 2, 0, "V")
+        quant_x(2, 0)
+        decode(1, 3, 1, "V")
+        exp(1, 1)
+        exp(1, 2)
+        decode(1, 3, 0, "V")
+        turn_x(3, 0, 0, "S")
+        encode(2, 1)
+        encode(2, 0)
+        encode(2, 2)
+        encode(2, 3)
+        turn_x(3, 1, 1, "S")
+        leaky(2, 0)
+        turn_x(3, 0, 1, "S")
+        keep_busy(1)
+        keep_busy(1)
+        quant_h(2, 0)
+        exp(1, 3)
+        quant_q(1)
+        leaky(2, 1)
+        turn_x(3, 1, 0, "S")
+        decode(2, 0, 1, "V")
+        quant_h(2, 1)
+        quant_x(3, 1)
+        decode(2, 1, 1, "V")
+        turn_q(2)
+        turn_h(2, 0, "S")
+        decode(2, 0, 0, "V")
+        turn_h(2, 1, "S")
+        exp(2, 0)
+        decode(2, 1, 0, "V")
+        decode(2, 2, 1, "V")
+        decode(2, 2, 0, "V")
+        quant_x(3, 0)
+        decode(2, 3, 1, "V")
+        exp(2, 1)
+        exp(2, 2)
+        decode(2, 3, 0, "V")
+        encode(3, 1)
+        encode(3, 0)
+        encode(3, 2)
+        encode(3, 3)
+        leaky(3, 0)
+        quant_h(3, 0)
+        exp(2, 3)
+        log(0, 0, 0, 1024)
+        quant_q(2)
+        finish(0, 0, 0, 1024)
+        leaky(3, 1)
+        log(0, 1, 0, 1024)
+        log(0, 2, 0, 1024)
+        finish(0, 1, 0, 1024)
+        finish(0, 2, 0, 1024)
+        decode(3, 0, 1, "V")
+        quant_h(3, 1)
+        log(0, 3, 0, 1024)
+        log(1, 0, 0, 1024)
+        log(1, 1, 0, 1024)
+        finish(0, 3, 0, 1024)
+        decode(3, 1, 1, "V")
+        turn_q(3)
+        finish(1, 0, 0, 1024)
+        decode(3, 0, 0, "V")
+        finish(1, 1, 0, 1024)
+        log(1, 2, 0, 1024)
+        decode(3, 1, 0, "V")
+        finish(1, 2, 0, 1024)
+        decode(3, 2, 1, "V")
+        decode(3, 2, 0, "V")
+        decode(3, 3, 1, "V")
+        log(1, 3, 0, 1024)
+        log(2, 0, 0, 1024)
+        decode(3, 3, 0, "V")
+        log(2, 1, 0, 1024)
+        finish(1, 3, 0, 1024)
+        quant_hc(2)
+        turn_h(3, 1, "V")
+        quant_hc(0)
+        log(2, 2, 0, 1024)
+        finish(2, 0, 0, 1024)
+        quant_q(3)
+        quant_hc(1)
+        log(2, 3, 0, 1024)
+        finish(2, 1, 0, 1024)
+        turn_h(3, 0, "V")
+        exp(3, 0)
+        finish(2, 2, 0, 1024)
+        exp(3, 1)
+        finish(2, 3, 0, 1024)
+        exp(3, 2)
+        quant_hc(3)
+        contrast(0)
+        contrast(1)
+        exp(3, 3)
+        log(3, 0, 0, 1024)
+        finish(3, 0, 0, 1024)
+        log(3, 1, 0, 1024)
+        log(3, 2, 0, 1024)
+        log(3, 3, 0, 512)
+        log(3, 3, 512, 1024)
+        finish(3, 1, 0, 1024)
+        finish(3, 2, 0, 1024)
+        finish(3, 3, 0, 512)
+        finish(3, 3, 512, 1024)

@@ -6,6 +6,7 @@ from concourse.masks import make_identity
 C, G, H, R = 2048, 1024, 512, 256
 FLOPS = 2 * C * G * H + 2 * C * H * G + 2 * R * C * H
 SLOPE = 0.1
+EARLY = 4
 TB, YB, DB = 3, 2, 3
 
 F32 = mybir.dt.float32
@@ -36,6 +37,8 @@ def tile_library_size_autoencoder_f6_kernel(
 
         lib_sb = keep.tile([P, GROUPS, PACK], BF16, name="lib_sb")
         nc.scalar.dma_start(out=lib_sb[:], in_=lib.rearrange("(g p s) -> p g s", p=P, s=PACK))
+        bdec_sb = keep.tile([P, 2, PACK], BF16, name="bdec_sb")
+        nc.scalar.dma_start(out=bdec_sb[:], in_=b_dec.rearrange("(h n m) -> n h m", h=2, m=PACK))
         benc_sb = keep.tile([P, PACK], BF16, name="benc_sb")
         nc.scalar.dma_start(out=benc_sb[:], in_=b_enc.rearrange("(p t) -> p t", t=PACK))
         wsc_sb = keep.tile([P, PACK], F32, name="wsc_sb")
@@ -49,7 +52,7 @@ def tile_library_size_autoencoder_f6_kernel(
         x_late = [keep.tile([P, 2, GROUP], BF16, name=f"x_late{half}") for half in range(2)]
         lib_first = keep.tile([P, GROUP], BF16, name="lib_first")
         lib_bc = keep.tile([P, C - GROUP], BF16, name="lib_bc")
-        bdec_bc = keep.tile([P, G], BF16, name="bdec_bc")
+        bdec_bc = [keep.tile([P, 512], BF16, name=f"bdec_bc{n}") for n in range(2)]
         unit_bc = keep.tile([P, H], BF16, name="unit_bc")
         x_sb = [None] + [keep.tile([P, PACK, G], BF16, name=f"x_sb{g}") for g in range(1, GROUPS)]
         w_raw = [work.tile([P, PACK, H], BF16, name="w_raw", align_bytes=256) for c in range(KP)]
@@ -64,10 +67,9 @@ def tile_library_size_autoencoder_f6_kernel(
             )
         nc.sync.dma_start(out=wd_bytes[:], in_=w_dec_bytes.rearrange("(p t) g -> p t g", t=PACK))
         nc.sync.dma_start(out=x_sb[1][:], in_=x_view[1])
-        nc.sync.dma_start(out=bdec_bc[:], in_=b_dec.partition_broadcast(P))
-        nc.sync.dma_start(out=q_sb[:], in_=q.rearrange("(b r) c -> r b c", r=P))
         nc.sync.dma_start(out=x_sb[2][:], in_=x_view[2])
         nc.sync.dma_start(out=lib_bc[:], in_=lib[GROUP:C].partition_broadcast(P))
+        nc.sync.dma_start(out=q_sb[:], in_=q.rearrange("(b r) c -> r b c", r=P))
         nc.sync.dma_start(out=x_sb[3][:], in_=x_view[3])
         nc.sync.dma_start(out=unit_bc[:], in_=unit.partition_broadcast(P))
 
@@ -89,13 +91,20 @@ def tile_library_size_autoencoder_f6_kernel(
                 bank = psum.tile([P, 512], F32, name="d_bank", bufs=DB)
                 nc.tensor.matmul(out=bank[:], lhsT=ident16[:], rhs=dummy_in[:], start=True, stop=True)
 
-        def spread(columns, out):
+        def spread(which):
+            columns = lib_sb[:, 0, :] if which == 0 else bdec_sb[:, which - 1, :]
             bank = psum.tile([P, PACK, P], F32, name="tp", bufs=TB)
             for m in range(PACK):
                 nc.tensor.matmul(
                     out=bank[:, m, :], lhsT=columns[:, m : m + 1].to_broadcast([P, P]), rhs=ident16[:], start=True, stop=True
                 )
-            nc.scalar.copy(out=out.rearrange("p (m n) -> p m n", m=PACK), in_=bank[:])
+            if which == 0:
+                nc.scalar.copy(out=lib_first[:].rearrange("p (m n) -> p m n", m=PACK), in_=bank[:])
+            else:
+                nc.scalar.copy(
+                    out=bdec_bc[which - 1][:].rearrange("p (n m) -> p n m", m=PACK),
+                    in_=bank[:].rearrange("p m n -> p n m"),
+                )
 
         x_grouped = {}
         x_codes, x_scales = {}, {}
@@ -238,7 +247,7 @@ def tile_library_size_autoencoder_f6_kernel(
 
         z = {}
 
-        def decode(g, s, n, engine="V"):
+        def decode(g, s, n):
             bank = psum.tile([P, 512], F32, name="d_bank", bufs=DB)
             nc.tensor.matmul_mx(
                 out=bank[:],
@@ -249,30 +258,53 @@ def tile_library_size_autoencoder_f6_kernel(
                 start=True,
                 stop=True,
             )
-            if (g, s) not in z:
-                z[g, s] = keep.tile([P, G], F32, name=f"z{g}_{s}")
+            if (g, s // 2) not in z:
+                z[g, s // 2] = keep.tile([P, 2, G], F32, name=f"z{g}_{s // 2}")
             nc.vector.scalar_tensor_tensor(
-                out=z[g, s][:, n * 512 : (n + 1) * 512],
+                out=z[g, s // 2][:, s % 2, n * 512 : (n + 1) * 512],
                 in0=bank[:],
                 scalar=invlib[:, g, s : s + 1],
-                in1=bdec_bc[:, n * 512 : (n + 1) * 512],
+                in1=bdec_bc[n][:],
                 op0=ALU.mult,
                 op1=ALU.add,
             )
 
-        def exp(g, s):
-            nc.scalar.activation(out=z[g, s][:], in_=z[g, s][:], func=ACT.Exp)
+        def exp(g, half):
+            nc.scalar.activation(out=z[g, half][:], in_=z[g, half][:], func=ACT.Exp)
 
-        def log(g, s, lo=0, hi=G):
-            nc.scalar.activation(out=z[g, s][:, lo:hi], in_=z[g, s][:, lo:hi], func=ACT.Ln, bias=1.0)
+        mean_view = out_mean.rearrange("(g p s) n -> g p s n", p=P, s=PACK)
 
-        mean_view = out_mean.rearrange("(g p s) n -> g s p n", p=P, s=PACK)
+        def log(g, half):
+            if 2 * g + half < EARLY:
+                pieces = [(0, 2, 0, G)]
+            elif (g, half) != (GROUPS - 1, 1):
+                pieces = [(0, 1, 0, G), (1, 2, 0, G)]
+            else:
+                pieces = [(0, 1, 0, G), (1, 2, 0, 512), (1, 2, 512, G)]
+            for s0, s1, lo, hi in pieces:
+                part = z[g, half][:, s0:s1, lo:hi]
+                nc.scalar.activation(out=part, in_=part, func=ACT.Ln, bias=1.0)
 
-        def finish(g, s, lo=0, hi=G):
-            nc.vector.tensor_scalar(
-                out=z[g, s][:, lo:hi], in0=z[g, s][:, lo:hi], scalar1=depth_sb[:, g, s : s + 1], scalar2=None, op0=ALU.mult
-            )
-            nc.sync.dma_start(out=mean_view[g, s][:, lo:hi], in_=z[g, s][:, lo:hi])
+        def finish(g, half):
+            if 2 * g + half < EARLY:
+                pieces = [(0, 2, 0, G)]
+            elif (g, half) != (GROUPS - 1, 1):
+                pieces = [(0, 1, 0, G), (1, 2, 0, G)]
+            else:
+                pieces = [(0, 1, 0, G), (1, 2, 0, 512), (1, 2, 512, G)]
+            for s0, s1, lo, hi in pieces:
+                for s in range(s0, s1):
+                    part = z[g, half][:, s, lo:hi]
+                    nc.vector.tensor_scalar(
+                        out=part,
+                        in0=part,
+                        scalar1=depth_sb[:, g, 2 * half + s : 2 * half + s + 1],
+                        scalar2=None,
+                        op0=ALU.mult,
+                    )
+                nc.sync.dma_start(
+                    out=mean_view[g][:, 2 * half + s0 : 2 * half + s1, lo:hi], in_=z[g, half][:, s0:s1, lo:hi]
+                )
 
         hc_grouped, hc_codes, hc_scales = {}, {}, {}
 
@@ -339,195 +371,172 @@ def tile_library_size_autoencoder_f6_kernel(
             nc.sync.dma_start(out=out_contrast[b * P : (b + 1) * P, :], in_=res[:])
 
         group_w(1, 0, 4, "V")
-        keep_busy(1)
-        keep_busy(1)
+        spread(2)
+        group_w(0, 2, 4, "S")
         keep_busy(1)
         quant_w(1)
-        keep_busy(1)
-        spread(lib_sb[:, 0, :], lib_first[:])
-        keep_busy(1)
+        spread(1)
         keep_busy(1)
         keep_busy(1)
-        group_w(0, 2, 4, "S")
-        turn_x(0, 0, 0, "S")
+        keep_busy(1)
         turn_x(0, 0, 1, "S")
-        keep_busy(1)
         group_w(0, 0, 2, "V")
-        keep_busy(1)
-        quant_x(0, 0)
-        keep_busy(1)
         quant_w(0)
+        turn_x(0, 0, 0, "S")
+        keep_busy(1)
         widen_wd(0)
         turn_x(0, 1, 0, "S")
-        keep_busy(1)
         turn_x(0, 1, 1, "S")
+        spread(0)
+        widen_wd(1)
+        quant_x(0, 0)
+        group_wd(1, "S")
+        keep_busy(1)
         group_wd(0, "V")
         quant_x(0, 1, 2)
         keep_busy(1)
         keep_busy(1)
-        widen_wd(1)
-        keep_busy(1)
-        group_wd(1, "S")
-        keep_busy(1)
-        turn_x(1, 0, 0, "S")
-        encode(0, 1)
-        encode(0, 0)
-        encode(0, 2)
+        quant_wd(0)
         encode(0, 3)
-        turn_x(1, 1, 1, "S")
+        encode(0, 2)
+        encode(0, 0)
+        encode(0, 1)
+        turn_x(1, 1, 0, "S")
+        turn_x(1, 0, 0, "S")
         leaky(0, 0)
-        turn_x(1, 0, 1, "S")
         keep_busy(1)
         quant_wd(1)
         keep_busy(1)
         quant_h(0, 0)
-        quant_wd(0)
+        turn_x(1, 1, 1, "S")
         leaky(0, 1)
-        turn_x(1, 1, 0, "S")
-        decode(0, 0, 1, "V")
-        quant_h(0, 1)
-        quant_x(1, 1)
-        decode(0, 1, 1, "V")
-        turn_q(0)
-        turn_h(0, 0, "S")
-        decode(0, 0, 0, "V")
-        turn_h(0, 1, "S")
-        exp(0, 0)
-        decode(0, 1, 0, "V")
-        decode(0, 2, 1, "V")
-        decode(0, 2, 0, "V")
-        quant_x(1, 0)
-        decode(0, 3, 1, "V")
-        exp(0, 1)
-        exp(0, 2)
-        decode(0, 3, 0, "V")
-        turn_x(2, 0, 0, "S")
-        encode(1, 1)
-        encode(1, 0)
-        encode(1, 2)
-        encode(1, 3)
+        turn_x(1, 0, 1, "S")
+        decode(0, 1, 1)
+        decode(0, 0, 1)
         turn_x(2, 1, 1, "S")
-        leaky(1, 0)
+        quant_x(1, 0)
+        turn_h(0, 0, "S")
+        decode(0, 0, 0)
+        quant_x(1, 1)
+        quant_h(0, 1)
+        decode(0, 1, 0)
+        turn_h(0, 1, "S")
         turn_x(2, 0, 1, "S")
-        keep_busy(1)
-        keep_busy(1)
-        quant_h(1, 0)
-        exp(0, 3)
-        quant_q(0)
-        leaky(1, 1)
+        encode(1, 2)
+        decode(0, 3, 0)
+        encode(1, 3)
+        exp(0, 0)
         turn_x(2, 1, 0, "S")
-        decode(1, 0, 1, "V")
-        quant_h(1, 1)
-        quant_x(2, 1)
-        decode(1, 1, 1, "V")
-        turn_q(1)
-        turn_h(1, 0, "S")
-        decode(1, 0, 0, "V")
-        turn_h(1, 1, "S")
-        exp(1, 0)
-        decode(1, 1, 0, "V")
-        decode(1, 2, 1, "V")
-        decode(1, 2, 0, "V")
-        quant_x(2, 0)
-        decode(1, 3, 1, "V")
-        exp(1, 1)
-        exp(1, 2)
-        decode(1, 3, 0, "V")
-        turn_x(3, 0, 0, "S")
-        encode(2, 1)
-        encode(2, 0)
-        encode(2, 2)
-        encode(2, 3)
-        turn_x(3, 1, 1, "S")
-        leaky(2, 0)
-        turn_x(3, 0, 1, "S")
+        decode(0, 2, 0)
+        decode(0, 2, 1)
+        encode(1, 0)
+        encode(1, 1)
+        decode(0, 3, 1)
+        leaky(1, 0)
+        turn_q(0)
+        turn_x(2, 0, 0, "S")
         keep_busy(1)
+        exp(0, 1)
+        quant_h(1, 0)
+        keep_busy(1)
+        turn_x(3, 1, 1, "S")
+        leaky(1, 1)
+        turn_q(1)
+        decode(1, 0, 0)
+        decode(1, 1, 1)
+        turn_h(1, 0, "S")
+        quant_h(1, 1)
+        decode(1, 0, 1)
+        decode(1, 1, 0)
+        turn_x(3, 0, 0, "S")
+        quant_x(2, 0)
+        turn_x(3, 0, 1, "S")
+        exp(1, 0)
+        decode(1, 2, 1)
+        decode(1, 3, 0)
+        quant_x(2, 1)
+        turn_h(1, 1, "S")
+        turn_x(3, 1, 0, "S")
+        decode(1, 3, 1)
+        decode(1, 2, 0)
+        encode(2, 3)
+        quant_q(0)
+        encode(2, 2)
+        quant_x(3, 1)
+        encode(2, 0)
+        encode(2, 1)
+        exp(1, 1)
+        quant_x(3, 0)
+        log(0, 1)
+        log(1, 1)
+        leaky(2, 1)
+        quant_q(1)
+        quant_h(2, 1)
+        turn_q(2)
+        keep_busy(1)
+        log(1, 0)
+        leaky(2, 0)
+        encode(3, 0)
+        decode(2, 3, 1)
+        encode(3, 2)
+        finish(0, 1)
+        encode(3, 1)
+        encode(3, 3)
+        log(0, 0)
         keep_busy(1)
         quant_h(2, 0)
-        exp(1, 3)
-        quant_q(1)
-        leaky(2, 1)
-        turn_x(3, 1, 0, "S")
-        decode(2, 0, 1, "V")
-        quant_h(2, 1)
-        quant_x(3, 1)
-        decode(2, 1, 1, "V")
-        turn_q(2)
-        turn_h(2, 0, "S")
-        decode(2, 0, 0, "V")
-        turn_h(2, 1, "S")
-        exp(2, 0)
-        decode(2, 1, 0, "V")
-        decode(2, 2, 1, "V")
-        decode(2, 2, 0, "V")
-        quant_x(3, 0)
-        decode(2, 3, 1, "V")
-        exp(2, 1)
-        exp(2, 2)
-        decode(2, 3, 0, "V")
-        encode(3, 1)
-        encode(3, 0)
-        encode(3, 2)
-        encode(3, 3)
+        keep_busy(1)
         leaky(3, 0)
+        keep_busy(1)
+        decode(2, 0, 1)
+        decode(2, 0, 0)
+        turn_h(2, 1, "S")
         quant_h(3, 0)
-        exp(2, 3)
-        log(0, 0, 0, 1024)
-        quant_q(2)
-        finish(0, 0, 0, 1024)
+        decode(2, 1, 1)
+        decode(2, 2, 1)
+        decode(2, 1, 0)
+        turn_h(2, 0, "S")
         leaky(3, 1)
-        log(0, 1, 0, 1024)
-        log(0, 2, 0, 1024)
-        finish(0, 1, 0, 1024)
-        finish(0, 2, 0, 1024)
-        decode(3, 0, 1, "V")
+        decode(3, 0, 0)
+        keep_busy(1)
         quant_h(3, 1)
-        log(0, 3, 0, 1024)
-        log(1, 0, 0, 1024)
-        log(1, 1, 0, 1024)
-        finish(0, 3, 0, 1024)
-        decode(3, 1, 1, "V")
-        turn_q(3)
-        finish(1, 0, 0, 1024)
-        decode(3, 0, 0, "V")
-        finish(1, 1, 0, 1024)
-        log(1, 2, 0, 1024)
-        decode(3, 1, 0, "V")
-        finish(1, 2, 0, 1024)
-        decode(3, 2, 1, "V")
-        decode(3, 2, 0, "V")
-        decode(3, 3, 1, "V")
-        log(1, 3, 0, 1024)
-        log(2, 0, 0, 1024)
-        decode(3, 3, 0, "V")
-        log(2, 1, 0, 1024)
-        finish(1, 3, 0, 1024)
+        exp(2, 0)
+        decode(2, 3, 0)
+        decode(3, 1, 0)
+        decode(2, 2, 0)
+        decode(3, 3, 0)
+        decode(3, 1, 1)
+        decode(3, 0, 1)
+        decode(3, 2, 1)
+        finish(1, 1)
+        decode(3, 3, 1)
+        exp(2, 1)
+        keep_busy(1)
+        decode(3, 2, 0)
         quant_hc(2)
-        turn_h(3, 1, "V")
-        quant_hc(0)
-        log(2, 2, 0, 1024)
-        finish(2, 0, 0, 1024)
-        quant_q(3)
-        quant_hc(1)
-        log(2, 3, 0, 1024)
-        finish(2, 1, 0, 1024)
-        turn_h(3, 0, "V")
         exp(3, 0)
-        finish(2, 2, 0, 1024)
+        finish(1, 0)
+        keep_busy(1)
         exp(3, 1)
-        finish(2, 3, 0, 1024)
-        exp(3, 2)
+        log(2, 0)
+        quant_q(2)
+        quant_hc(1)
+        finish(0, 0)
+        keep_busy(1)
+        log(2, 1)
+        turn_h(3, 1, "V")
+        turn_h(3, 0, "V")
+        finish(2, 0)
+        quant_hc(0)
+        turn_q(3)
+        log(3, 0)
+        finish(2, 1)
+        keep_busy(1)
+        quant_q(3)
+        keep_busy(1)
+        log(3, 1)
         quant_hc(3)
-        contrast(0)
+        finish(3, 0)
         contrast(1)
-        exp(3, 3)
-        log(3, 0, 0, 1024)
-        finish(3, 0, 0, 1024)
-        log(3, 1, 0, 1024)
-        log(3, 2, 0, 1024)
-        log(3, 3, 0, 512)
-        log(3, 3, 512, 1024)
-        finish(3, 1, 0, 1024)
-        finish(3, 2, 0, 1024)
-        finish(3, 3, 0, 512)
-        finish(3, 3, 512, 1024)
+        contrast(0)
+        finish(3, 1)

from contextlib import ExitStack

import concourse.mybir as mybir
from concourse.masks import make_identity

C, G, H, R = 2048, 1024, 512, 256
FLOPS = 2 * C * G * H + 2 * C * H * G + 2 * R * C * H
SLOPE = 0.1
EARLY = 4
TB, YB, DB = 3, 2, 3

F32 = mybir.dt.float32
BF16 = mybir.dt.bfloat16
U32 = mybir.dt.uint32
U8 = mybir.dt.uint8
E4M3 = mybir.dt.float8_e4m3fn
FP8X4 = mybir.dt.float8_e4m3fn_x4
ALU = mybir.AluOpType
ACT = mybir.ActivationFunctionType

P = 128
PACK = 4
GROUP = P * PACK
GROUPS = C // GROUP
KP = G // GROUP


def tile_library_size_autoencoder_f6_kernel(
    tc, x, lib, w_enc, b_enc, w_dec_bytes, w_dec_scale, b_dec, depth, q, unit, out_mean, out_contrast
):
    nc = tc.nc
    with ExitStack() as ctx:
        keep = ctx.enter_context(tc.tile_pool(name="keep", bufs=1))
        work = ctx.enter_context(tc.tile_pool(name="work", bufs=2))
        psum = ctx.enter_context(tc.psum_pool(name="psum", bufs=2))
        ctx.enter_context(tc.manual_schedule())

        lib_sb = keep.tile([P, GROUPS, PACK], BF16, name="lib_sb")
        nc.scalar.dma_start(out=lib_sb[:], in_=lib.rearrange("(g p s) -> p g s", p=P, s=PACK))
        bdec_sb = keep.tile([P, 2, PACK], BF16, name="bdec_sb")
        nc.scalar.dma_start(out=bdec_sb[:], in_=b_dec.rearrange("(h n m) -> n h m", h=2, m=PACK))
        benc_sb = keep.tile([P, PACK], BF16, name="benc_sb")
        nc.scalar.dma_start(out=benc_sb[:], in_=b_enc.rearrange("(p t) -> p t", t=PACK))
        wsc_sb = keep.tile([P, PACK], F32, name="wsc_sb")
        nc.scalar.dma_start(out=wsc_sb[:], in_=w_dec_scale.rearrange("(p t) o -> p (t o)", t=PACK))
        depth_sb = keep.tile([P, GROUPS, PACK], BF16, name="depth_sb")
        nc.scalar.dma_start(out=depth_sb[:], in_=depth.rearrange("(g p s) -> p g s", p=P, s=PACK))

        x_view = x.rearrange("(g p s) k -> g p s k", p=P, s=PACK)
        w_view = w_enc.rearrange("(c p j) n -> c p j n", p=P, j=PACK)
        x_first = [keep.tile([P, PACK, GROUP], BF16, name="x_first")]
        x_late = [keep.tile([P, 2, GROUP], BF16, name=f"x_late{half}") for half in range(2)]
        lib_first = keep.tile([P, GROUP], BF16, name="lib_first")
        lib_bc = keep.tile([P, C - GROUP], BF16, name="lib_bc")
        bdec_bc = [keep.tile([P, 512], BF16, name=f"bdec_bc{n}") for n in range(2)]
        unit_bc = keep.tile([P, H], BF16, name="unit_bc")
        x_sb = [None] + [keep.tile([P, PACK, G], BF16, name=f"x_sb{g}") for g in range(1, GROUPS)]
        w_raw = [work.tile([P, PACK, H], BF16, name="w_raw", align_bytes=256) for c in range(KP)]
        wd_bytes = keep.tile([P, PACK, G], U8, name="wd_bytes")
        q_sb = keep.tile([P, 2, C], BF16, name="q_sb")
        for c in range(KP):
            nc.sync.dma_start(out=w_raw[c][:], in_=w_view[c])
        nc.sync.dma_start(out=x_first[0][:], in_=x_view[0][:, :, 0:GROUP])
        for half in range(2):
            nc.sync.dma_start(
                out=x_late[half][:], in_=x_view[0][:, 2 * half : 2 * half + 2, GROUP:G]
            )
        nc.sync.dma_start(out=wd_bytes[:], in_=w_dec_bytes.rearrange("(p t) g -> p t g", t=PACK))
        nc.sync.dma_start(out=x_sb[1][:], in_=x_view[1])
        nc.sync.dma_start(out=x_sb[2][:], in_=x_view[2])
        nc.sync.dma_start(out=lib_bc[:], in_=lib[GROUP:C].partition_broadcast(P))
        nc.sync.dma_start(out=q_sb[:], in_=q.rearrange("(b r) c -> r b c", r=P))
        nc.sync.dma_start(out=x_sb[3][:], in_=x_view[3])
        nc.sync.dma_start(out=unit_bc[:], in_=unit.partition_broadcast(P))

        ident32 = keep.tile([P, P], F32, name="ident32")
        make_identity(nc, ident32[:])
        ident16 = keep.tile([P, P], BF16, name="ident16")
        make_identity(nc, ident16[:])
        warm = keep.tile([P, 1], F32, name="warm")
        nc.vector.memset(warm[:], 0.0)
        nc.scalar.activation(out=warm[:], in_=warm[:], func=ACT.Exp)
        invlib = keep.tile([P, GROUPS, PACK], F32, name="invlib")
        nc.vector.reciprocal(out=invlib[:], in_=lib_sb[:])

        dummy_in = keep.tile([P, 512], BF16, name="dummy_in")
        nc.vector.memset(dummy_in[:], 0.0)

        def keep_busy(n):
            for i in range(n):
                bank = psum.tile([P, 512], F32, name="d_bank", bufs=DB)
                nc.tensor.matmul(out=bank[:], lhsT=ident16[:], rhs=dummy_in[:], start=True, stop=True)

        def spread(which):
            columns = lib_sb[:, 0, :] if which == 0 else bdec_sb[:, which - 1, :]
            bank = psum.tile([P, PACK, P], F32, name="tp", bufs=TB)
            for m in range(PACK):
                nc.tensor.matmul(
                    out=bank[:, m, :], lhsT=columns[:, m : m + 1].to_broadcast([P, P]), rhs=ident16[:], start=True, stop=True
                )
            if which == 0:
                nc.scalar.copy(out=lib_first[:].rearrange("p (m n) -> p m n", m=PACK), in_=bank[:])
            else:
                nc.scalar.copy(
                    out=bdec_bc[which - 1][:].rearrange("p (n m) -> p n m", m=PACK),
                    in_=bank[:].rearrange("p m n -> p n m"),
                )

        x_grouped = {}
        x_codes, x_scales = {}, {}
        we_codes = [keep.tile([P, H], U32, name=f"we_codes{c}", align_bytes=256) for c in range(KP)]
        we_scales = [keep.tile([P, H], U8, name=f"we_scales{c}", align_bytes=256) for c in range(KP)]
        wd_codes = keep.tile([P, G], U32, name="wd_codes", align_bytes=256)
        wd_scales = keep.tile([P, G], U8, name="wd_scales", align_bytes=256)

        def turn_x(g, c, half, engine):
            bank = psum.tile([P, 2, 2 * P], F32, name="tp", bufs=TB)
            if g > 0:
                words = x_sb[g][:, 2 * half : 2 * half + 2, c * GROUP : (c + 1) * GROUP].bitcast(F32)
            elif c == 0:
                words = x_first[0][:, 2 * half : 2 * half + 2, :].bitcast(F32)
            else:
                words = x_late[half][:].bitcast(F32)
            for u in (0, 1):
                for s in (0, 1):
                    nc.tensor.transpose(
                        bank[:, u, s * P : (s + 1) * P],
                        words[:, s, u : 2 * P : 2],
                        ident32[:],
                    )
            if (g, c) not in x_grouped:
                x_grouped[g, c] = work.tile([P, GROUP, PACK], BF16, name=f"x_grouped{c}", align_bytes=256)
            dst = x_grouped[g, c][:].bitcast(F32)[:, half * 256 : (half + 1) * 256, :]
            src = bank[:].rearrange("p u c -> p c u")
            if engine == "S":
                nc.scalar.copy(out=dst, in_=src)
            else:
                nc.vector.tensor_copy(out=dst, in_=src)

        def quant_x(g, c, parts=1):
            x_codes[g, c] = work.tile([P, GROUP], U32, name=f"x_codes{c}", align_bytes=256)
            x_scales[g, c] = work.tile([P, GROUP], U8, name=f"x_scales{c}", align_bytes=256)
            width = GROUP // parts
            for i in range(parts):
                cols = slice(i * width, (i + 1) * width)
                nc.vector.quantize_mx(
                    out=x_codes[g, c][:, cols].bitcast(FP8X4),
                    scales=x_scales[g, c][:, cols],
                    in_=x_grouped[g, c][:, cols, :].rearrange("p c j -> p (c j)"),
                )

        w_grouped = {}

        def group_w(c, lo, hi, engine):
            if c not in w_grouped:
                w_grouped[c] = work.tile([P, H, PACK], BF16, name="w_grouped", align_bytes=256)
            dst = w_grouped[c][:].rearrange("p (t m) j -> p t m j", t=PACK)[:, lo:hi]
            src = w_raw[c][:].rearrange("p j (m t) -> p t m j", t=PACK)[:, lo:hi]
            if engine == "S":
                nc.scalar.copy(out=dst, in_=src)
            else:
                nc.vector.tensor_copy(out=dst, in_=src)

        def quant_w(c):
            nc.vector.quantize_mx(
                out=we_codes[c][:].bitcast(FP8X4), scales=we_scales[c][:], in_=w_grouped[c][:].rearrange("p c j -> p (c j)")
            )

        wd_wide = [keep.tile([P, PACK, 512], BF16, name=f"wd_wide{n}") for n in range(2)]
        wd_grouped = {}

        def widen_wd(n):
            cols = slice(n * 512, (n + 1) * 512)
            for t in range(PACK):
                nc.scalar.activation(
                    out=wd_wide[n][:, t, :],
                    in_=wd_bytes[:, t, cols].bitcast(E4M3),
                    func=ACT.Copy,
                    scale=wsc_sb[:, t : t + 1],
                )

        def group_wd(n, engine):
            wd_grouped[n] = work.tile([P, H, PACK], BF16, name="w_grouped", align_bytes=256)
            src = wd_wide[n][:].rearrange("p t g -> p g t")
            if engine == "S":
                nc.scalar.copy(out=wd_grouped[n][:], in_=src)
            else:
                nc.vector.tensor_copy(out=wd_grouped[n][:], in_=src)

        def quant_wd(n):
            cols = slice(n * 512, (n + 1) * 512)
            nc.vector.quantize_mx(
                out=wd_codes[:, cols].bitcast(FP8X4),
                scales=wd_scales[:, cols],
                in_=wd_grouped[n][:].rearrange("p g t -> p (g t)"),
            )

        sums = {}
        h_grouped, h_codes, h_scales = {}, {}, {}

        def encode(g, t):
            bank = psum.tile([P, GROUP], F32, name="y_bank", bufs=YB)
            for c in range(KP):
                nc.tensor.matmul_mx(
                    out=bank[:],
                    lhsT=we_codes[c][:, t * P : (t + 1) * P].bitcast(FP8X4),
                    lhsT_scale=we_scales[c][:, t * P : (t + 1) * P],
                    rhs=x_codes[g, c][:].bitcast(FP8X4),
                    rhs_scale=x_scales[g, c][:],
                    start=(c == 0),
                    stop=(c == KP - 1),
                )
            if g not in sums:
                sums[g] = work.tile([P, PACK, GROUP], F32, name="sums", bufs=1)
            if g == 0:
                lib_row = lib_first[:].rearrange("p (s n) -> p s n", s=PACK)
            else:
                lib_row = lib_bc[:, (g - 1) * GROUP : g * GROUP].rearrange("p (n s) -> p s n", s=PACK)
            nc.vector.scalar_tensor_tensor(
                out=sums[g][:, t, :].rearrange("p (s n) -> p s n", s=PACK),
                in0=lib_row,
                scalar=benc_sb[:, t : t + 1],
                in1=bank[:].rearrange("p (s n) -> p s n", s=PACK),
                op0=ALU.mult,
                op1=ALU.add,
            )

        def leaky(g, part):
            if g not in h_grouped:
                h_grouped[g] = work.tile([P, GROUP, PACK], BF16, name="h_grouped", align_bytes=256)
            cols = slice(part * 256, (part + 1) * 256)
            src = sums[g][:, :, cols].rearrange("p t c -> p c t")
            nc.vector.scalar_tensor_tensor(
                out=h_grouped[g][:, cols, :], in0=src, scalar=SLOPE, in1=src, op0=ALU.mult, op1=ALU.max
            )

        def quant_h(g, part):
            if g not in h_codes:
                h_codes[g] = work.tile([P, GROUP], U32, name="h_codes", align_bytes=256)
                h_scales[g] = work.tile([P, GROUP], U8, name="h_scales", align_bytes=256)
            cols = slice(part * 256, (part + 1) * 256)
            nc.vector.quantize_mx(
                out=h_codes[g][:, cols].bitcast(FP8X4),
                scales=h_scales[g][:, cols],
                in_=h_grouped[g][:, cols, :].rearrange("p c t -> p (c t)"),
            )

        z = {}

        def decode(g, s, n):
            bank = psum.tile([P, 512], F32, name="d_bank", bufs=DB)
            nc.tensor.matmul_mx(
                out=bank[:],
                lhsT=h_codes[g][:, s * P : (s + 1) * P].bitcast(FP8X4),
                lhsT_scale=h_scales[g][:, s * P : (s + 1) * P],
                rhs=wd_codes[:, n * 512 : (n + 1) * 512].bitcast(FP8X4),
                rhs_scale=wd_scales[:, n * 512 : (n + 1) * 512],
                start=True,
                stop=True,
            )
            if (g, s // 2) not in z:
                z[g, s // 2] = keep.tile([P, 2, G], F32, name=f"z{g}_{s // 2}")
            nc.vector.scalar_tensor_tensor(
                out=z[g, s // 2][:, s % 2, n * 512 : (n + 1) * 512],
                in0=bank[:],
                scalar=invlib[:, g, s : s + 1],
                in1=bdec_bc[n][:],
                op0=ALU.mult,
                op1=ALU.add,
            )

        def exp(g, half):
            nc.scalar.activation(out=z[g, half][:], in_=z[g, half][:], func=ACT.Exp)

        mean_view = out_mean.rearrange("(g p s) n -> g p s n", p=P, s=PACK)

        def log(g, half):
            if 2 * g + half < EARLY:
                pieces = [(0, 2, 0, G)]
            elif (g, half) != (GROUPS - 1, 1):
                pieces = [(0, 1, 0, G), (1, 2, 0, G)]
            else:
                pieces = [(0, 1, 0, G), (1, 2, 0, 512), (1, 2, 512, G)]
            for s0, s1, lo, hi in pieces:
                part = z[g, half][:, s0:s1, lo:hi]
                nc.scalar.activation(out=part, in_=part, func=ACT.Ln, bias=1.0)

        def finish(g, half):
            if 2 * g + half < EARLY:
                pieces = [(0, 2, 0, G)]
            elif (g, half) != (GROUPS - 1, 1):
                pieces = [(0, 1, 0, G), (1, 2, 0, G)]
            else:
                pieces = [(0, 1, 0, G), (1, 2, 0, 512), (1, 2, 512, G)]
            for s0, s1, lo, hi in pieces:
                for s in range(s0, s1):
                    part = z[g, half][:, s, lo:hi]
                    nc.vector.tensor_scalar(
                        out=part,
                        in0=part,
                        scalar1=depth_sb[:, g, 2 * half + s : 2 * half + s + 1],
                        scalar2=None,
                        op0=ALU.mult,
                    )
                nc.sync.dma_start(
                    out=mean_view[g][:, 2 * half + s0 : 2 * half + s1, lo:hi], in_=z[g, half][:, s0:s1, lo:hi]
                )

        hc_grouped, hc_codes, hc_scales = {}, {}, {}

        def turn_h(g, tt, engine):
            bank = psum.tile([P, PACK, P], F32, name="tp", bufs=TB)
            words = h_grouped[g][:].bitcast(F32)
            for s in range(PACK):
                nc.tensor.transpose(bank[:, s, :], words[:, s * P : (s + 1) * P, tt : tt + 1].rearrange("p c o -> p (c o)"), ident32[:])
            if g not in hc_grouped:
                hc_grouped[g] = work.tile([P, H, PACK], BF16, name="w_raw" if g < 2 else "w_grouped", align_bytes=256)
            dst = hc_grouped[g][:, tt * 256 : (tt + 1) * 256, :]
            src = bank[:].bitcast(BF16).rearrange("p s c -> p c s")
            if engine == "S":
                nc.scalar.copy(out=dst, in_=src)
            else:
                nc.vector.tensor_copy(out=dst, in_=src)

        def quant_hc(g):
            hc_codes[g] = keep.tile([P, H], U32, name=f"hc_codes{g}", align_bytes=256)
            hc_scales[g] = keep.tile([P, H], U8, name=f"hc_scales{g}", align_bytes=256)
            nc.vector.quantize_mx(
                out=hc_codes[g][:].bitcast(FP8X4), scales=hc_scales[g][:], in_=hc_grouped[g][:].rearrange("p c j -> p (c j)")
            )

        q_grouped, q_codes, q_scales = {}, {}, {}

        def turn_q(g):
            bank = psum.tile([P, 2, 2 * P], F32, name="tp", bufs=TB)
            words = q_sb[:].bitcast(F32)
            for u in (0, 1):
                for b in (0, 1):
                    nc.tensor.transpose(
                        bank[:, u, b * P : (b + 1) * P], words[:, b, 256 * g + u : 256 * (g + 1) : 2], ident32[:]
                    )
            q_grouped[g] = work.tile([P, R, PACK], BF16, name="q_grouped", align_bytes=256, bufs=4)
            nc.scalar.copy(out=q_grouped[g][:].bitcast(F32), in_=bank[:].rearrange("p u c -> p c u"))

        def quant_q(g):
            q_codes[g] = keep.tile([P, R], U32, name=f"q_codes{g}", align_bytes=256)
            q_scales[g] = keep.tile([P, R], U8, name=f"q_scales{g}", align_bytes=256)
            nc.vector.quantize_mx(
                out=q_codes[g][:].bitcast(FP8X4), scales=q_scales[g][:], in_=q_grouped[g][:].rearrange("p c j -> p (c j)")
            )

        def contrast(b):
            bank = psum.tile([P, H], F32, name="d_bank", bufs=DB)
            for g in range(GROUPS):
                nc.tensor.matmul_mx(
                    out=bank[:],
                    lhsT=q_codes[g][:, b * P : (b + 1) * P].bitcast(FP8X4),
                    lhsT_scale=q_scales[g][:, b * P : (b + 1) * P],
                    rhs=hc_codes[g][:].bitcast(FP8X4),
                    rhs_scale=hc_scales[g][:],
                    start=(g == 0),
                    stop=(g == GROUPS - 1),
                )
            res = work.tile([P, H], F32, name="contrast_sb")
            nc.vector.tensor_tensor(
                out=res[:].rearrange("p (m v e) -> p m v e", v=2, e=2),
                in0=bank[:].rearrange("p (v m e) -> p m v e", v=2, e=2),
                in1=unit_bc[:].rearrange("p (m v e) -> p m v e", v=2, e=2),
                op=ALU.mult,
            )
            nc.sync.dma_start(out=out_contrast[b * P : (b + 1) * P, :], in_=res[:])

        group_w(1, 0, 4, "V")
        spread(2)
        group_w(0, 2, 4, "S")
        keep_busy(1)
        quant_w(1)
        spread(1)
        keep_busy(1)
        keep_busy(1)
        keep_busy(1)
        turn_x(0, 0, 1, "S")
        group_w(0, 0, 2, "V")
        quant_w(0)
        turn_x(0, 0, 0, "S")
        keep_busy(1)
        widen_wd(0)
        turn_x(0, 1, 0, "S")
        turn_x(0, 1, 1, "S")
        spread(0)
        widen_wd(1)
        quant_x(0, 0)
        group_wd(1, "S")
        keep_busy(1)
        group_wd(0, "V")
        quant_x(0, 1, 2)
        keep_busy(1)
        keep_busy(1)
        quant_wd(0)
        encode(0, 3)
        encode(0, 2)
        encode(0, 0)
        encode(0, 1)
        turn_x(1, 1, 0, "S")
        turn_x(1, 0, 0, "S")
        leaky(0, 0)
        keep_busy(1)
        quant_wd(1)
        keep_busy(1)
        quant_h(0, 0)
        turn_x(1, 1, 1, "S")
        leaky(0, 1)
        turn_x(1, 0, 1, "S")
        decode(0, 1, 1)
        decode(0, 0, 1)
        turn_x(2, 1, 1, "S")
        quant_x(1, 0)
        turn_h(0, 0, "S")
        decode(0, 0, 0)
        quant_x(1, 1)
        quant_h(0, 1)
        decode(0, 1, 0)
        turn_h(0, 1, "S")
        turn_x(2, 0, 1, "S")
        encode(1, 2)
        decode(0, 3, 0)
        encode(1, 3)
        exp(0, 0)
        turn_x(2, 1, 0, "S")
        decode(0, 2, 0)
        decode(0, 2, 1)
        encode(1, 0)
        encode(1, 1)
        decode(0, 3, 1)
        leaky(1, 0)
        turn_q(0)
        turn_x(2, 0, 0, "S")
        keep_busy(1)
        exp(0, 1)
        quant_h(1, 0)
        keep_busy(1)
        turn_x(3, 1, 1, "S")
        leaky(1, 1)
        turn_q(1)
        decode(1, 0, 0)
        decode(1, 1, 1)
        turn_h(1, 0, "S")
        quant_h(1, 1)
        decode(1, 0, 1)
        decode(1, 1, 0)
        turn_x(3, 0, 0, "S")
        quant_x(2, 0)
        turn_x(3, 0, 1, "S")
        exp(1, 0)
        decode(1, 2, 1)
        decode(1, 3, 0)
        quant_x(2, 1)
        turn_h(1, 1, "S")
        turn_x(3, 1, 0, "S")
        decode(1, 3, 1)
        decode(1, 2, 0)
        encode(2, 3)
        quant_q(0)
        encode(2, 2)
        quant_x(3, 1)
        encode(2, 0)
        encode(2, 1)
        exp(1, 1)
        quant_x(3, 0)
        log(0, 1)
        log(1, 1)
        leaky(2, 1)
        quant_q(1)
        quant_h(2, 1)
        turn_q(2)
        keep_busy(1)
        log(1, 0)
        leaky(2, 0)
        encode(3, 0)
        decode(2, 3, 1)
        encode(3, 2)
        finish(0, 1)
        encode(3, 1)
        encode(3, 3)
        log(0, 0)
        keep_busy(1)
        quant_h(2, 0)
        keep_busy(1)
        leaky(3, 0)
        keep_busy(1)
        decode(2, 0, 1)
        decode(2, 0, 0)
        turn_h(2, 1, "S")
        quant_h(3, 0)
        decode(2, 1, 1)
        decode(2, 2, 1)
        decode(2, 1, 0)
        turn_h(2, 0, "S")
        leaky(3, 1)
        decode(3, 0, 0)
        keep_busy(1)
        quant_h(3, 1)
        exp(2, 0)
        decode(2, 3, 0)
        decode(3, 1, 0)
        decode(2, 2, 0)
        decode(3, 3, 0)
        decode(3, 1, 1)
        decode(3, 0, 1)
        decode(3, 2, 1)
        finish(1, 1)
        decode(3, 3, 1)
        exp(2, 1)
        keep_busy(1)
        decode(3, 2, 0)
        quant_hc(2)
        exp(3, 0)
        finish(1, 0)
        keep_busy(1)
        exp(3, 1)
        log(2, 0)
        quant_q(2)
        quant_hc(1)
        finish(0, 0)
        keep_busy(1)
        log(2, 1)
        turn_h(3, 1, "V")
        turn_h(3, 0, "V")
        finish(2, 0)
        quant_hc(0)
        turn_q(3)
        log(3, 0)
        finish(2, 1)
        keep_busy(1)
        quant_q(3)
        keep_busy(1)
        log(3, 1)
        quant_hc(3)
        finish(3, 0)
        contrast(1)
        contrast(0)
        finish(3, 1)
